import numpy as np
import ml_dtypes


def mxq(x, axis, fmt="e4m3"):
    dtype, down = {"e4m3": (ml_dtypes.float8_e4m3fn, 7), "e5m2": (ml_dtypes.float8_e5m2, 14)}[fmt]
    v = np.moveaxis(np.asarray(x, np.float32).astype(ml_dtypes.bfloat16).astype(np.float64), axis, -1)
    blocks = v.reshape(v.shape[:-1] + (-1, 32))
    amax = np.abs(blocks).max(-1, keepdims=True)
    byte = np.maximum(np.where(amax > 0, np.frexp(amax)[1] - 1 + 127, 0) - down, 1)
    scale = np.exp2(byte - 127.0)
    codes = (blocks / scale).astype(np.float32).astype(dtype).astype(np.float64)
    return np.moveaxis((codes * scale).reshape(v.shape), -1, axis)


WIDE = False


def mx_kscale(k):
    if not WIDE:
        return np.ones(k)
    levels = np.array([10, -10, 5, -5, 0])
    if k % 512:
        return np.exp2(np.random.permutation(np.resize(levels, k // 32))).repeat(32)
    a = np.empty((k // 512, 16))
    for p in range(k // 512):
        a[p, :8] = np.random.permutation(np.resize(levels, 8))
        for g in range(8):
            far = levels[np.abs(levels - a[p, g]) >= 10]
            a[p, g + 8] = far[np.random.randint(len(far))]
    return np.exp2(a.ravel()).repeat(32)


def f64(x):
    return np.asarray(x).astype(np.float64)


def striped8(idx):
    return np.asarray(idx).reshape(8, -1, 16).transpose(0, 2, 1).reshape(128, -1).astype(np.uint16)


def unstriped8(offs):
    return offs.reshape(8, 16, -1).transpose(0, 2, 1).reshape(8, -1).astype(np.int64)


def pick8(x, idx, run):
    r = np.arange(len(x))
    return x[r[:, None], idx[r % (8 * run) // run]]


E2M1 = np.array([0.0, 0.5, 1.0, 1.5, 2.0, 3.0, 4.0, 6.0, -0.0, -0.5, -1.0, -1.5, -2.0, -3.0, -4.0, -6.0])


def pack_weight(w, fmt):
    k, n = w.shape
    w = f64(np.asarray(w, np.float32).astype(ml_dtypes.bfloat16)).reshape(k // 32, 32, n)
    amax = np.abs(w).max(1)
    if fmt == "e4m3":
        byte = np.frexp(amax)[1] - 1 + 127 - 7
    else:
        mant, ex = np.frexp(amax / 6.0)
        byte = np.where(mant > 0.5, ex, ex - 1) + 127
    byte = np.clip(np.where(amax > 0, byte, 1), 1, 254)
    scaled = (w * np.exp2(127.0 - byte)[:, None, :]).reshape(k, n).astype(np.float32)
    by_word = np.ascontiguousarray(scaled.reshape(k // 512, 128, 4, n).transpose(0, 1, 3, 2))
    if fmt == "e4m3":
        words = by_word.astype(ml_dtypes.float8_e4m3fn).view(np.uint8)
    else:
        c = by_word.astype(ml_dtypes.float4_e2m1fn).view(np.uint8) & 0xF
        words = (c[..., 0::2] | (c[..., 1::2] << 4)).reshape(k // 512, 128, 2 * n)
    return np.ascontiguousarray(words), np.ascontiguousarray(byte.astype(np.uint8).reshape(k // 512, 16, n))


def unpack_weight(words, scales, fmt):
    g, _, n = scales.shape
    words = np.ascontiguousarray(words).reshape(g, 128, n, -1)
    if fmt == "e4m3":
        vals = words.view(ml_dtypes.float8_e4m3fn).astype(np.float64)
    else:
        nib = np.empty((g, 128, n, 4), np.uint8)
        nib[..., 0::2] = words & 0xF
        nib[..., 1::2] = words >> 4
        vals = E2M1[nib]
    vals = vals * np.repeat(np.exp2(scales.astype(np.float64) - 127.0), 8, axis=1)[..., None]
    return vals.transpose(0, 1, 3, 2).reshape(g * 512, n)


D, T, I, Q, E = 512, 1024, 512, 512, 256


def setup_inputs():
    n = np.random.standard_normal
    idx = np.stack([np.random.permutation(T)[:I] for _ in range(8)])
    idx2 = np.stack([np.random.permutation(T)[:I] for _ in range(8)])
    idx3 = np.stack([np.random.permutation(T)[:I] for _ in range(8)])
    idx4 = np.stack([np.random.permutation(T)[:I] for _ in range(8)])
    idx5 = np.stack([np.random.permutation(T)[:I] for _ in range(8)])
    idx6 = np.stack([np.random.permutation(T)[:I] for _ in range(8)])
    fd = mx_kscale(D)
    fq = mx_kscale(Q)
    keysp = pack_weight(n((D, T)) / fd[:, None], "e2m1")
    mixp = pack_weight(n((Q, E)) * 1.0 / np.sqrt(Q) / fq[:, None], "e4m3")
    return {
        "query": (n((D, Q)) * 1.0 / np.sqrt(D) * fd[:, None]).astype(np.float32),
        "keys_words": keysp[0],
        "keys_scales": keysp[1],
        "rowf": (np.random.uniform(0.5, 2.0, (Q, 1)) * fq[:, None]).astype(np.float32),
        "mix_words": mixp[0],
        "mix_scales": mixp[1],
        "offs": striped8(idx),
        "offs2": striped8(idx2),
        "offs3": striped8(idx3),
        "offs4": striped8(idx4),
        "offs5": striped8(idx5),
        "offs6": striped8(idx6),
    }


def reference(query, keys_words, keys_scales, rowf, mix_words, mix_scales, offs, offs2, offs3, offs4, offs5, offs6):
    idx = unstriped8(offs)
    idx2 = unstriped8(offs2)
    idx3 = unstriped8(offs3)
    idx4 = unstriped8(offs4)
    idx5 = unstriped8(offs5)
    idx6 = unstriped8(offs6)
    keysu = unpack_weight(keys_words, keys_scales, "e2m1")
    mixu = unpack_weight(mix_words, mix_scales, "e4m3")
    queryq = mxq(f64(query), 0, "e4m3")
    a = queryq.T @ keysu
    f1 = np.zeros((Q, T))
    f1[np.arange(Q)[:, None], idx2[np.arange(Q) % 512 // 64]] = pick8(a, idx, 64)
    c1 = np.maximum(a, f1)
    w = pick8(c1, idx3, 64) - pick8(c1, idx4, 64)
    f2 = np.zeros((Q, T))
    f2[np.arange(Q)[:, None], idx5[np.arange(Q) % 512 // 64]] = w
    c2 = c1 + f2
    g = pick8(c2, idx6, 64)
    gw = g * f64(rowf)
    gwq = mxq(gw, 0, "e4m3")
    y = mixu.T @ gwq
    return y

@@ -1,0 +1,205 @@
+from contextlib import ExitStack
+
+import concourse.mybir as mybir
+
+D, T, I, Q, E = 512, 1024, 512, 512, 256
+FLOPS = 2 * D * Q * T + 2 * Q * E * I
+
+F32 = mybir.dt.float32
+BF16 = mybir.dt.bfloat16
+I32 = mybir.dt.int32
+U32 = mybir.dt.uint32
+U16 = mybir.dt.uint16
+U8 = mybir.dt.uint8
+FP8X4 = mybir.dt.float8_e4m3fn_x4
+FP4X4 = mybir.dt.float4_e2m1fn_x4
+ALU = mybir.AluOpType
+COPY = mybir.ActivationFunctionType.Copy
+
+P = 128
+PACK = 4
+BANK = 512
+HALF = I // 2
+LIST_COLS = I // 16
+
+
+def tile_attend_hopmax_one_mixed_kernel(
+    tc, query, keys_words, keys_scales, rowf, mix_words, mix_scales, offs, offs2, offs3, offs4, offs5, offs6, out
+):
+    nc = tc.nc
+    with ExitStack() as ctx:
+        keep = ctx.enter_context(tc.tile_pool(name="keep", bufs=1))
+        shared = ctx.enter_context(tc.tile_pool(name="shared", bufs=1))
+        psum = ctx.enter_context(tc.psum_pool(name="psum", bufs=1))
+
+        lists = [keep.tile([P, LIST_COLS], U16, name="list%d" % n) for n in range(6)]
+        key_scale = keep.tile([P, T], U8, align_bytes=64)
+        key_words = keep.tile([P, 2 * T], U8, align_bytes=64)
+        mix_scale = keep.tile([P, E], U8, align_bytes=64)
+        mix_codes = keep.tile([P, E], U32, align_bytes=64)
+        row_factor = keep.tile([P, PACK], F32)
+        raw = [keep.tile([P, PACK, Q // 2], F32, name="raw%d" % c) for c in range(2)]
+        f1 = [keep.tile([P, T], F32, name="f1_%d" % b) for b in range(2)]
+        f2 = [keep.tile([P, T], F32, name="f2_%d" % b) for b in range(2)]
+
+        nc.vector.memset(key_scale[:].bitcast(I32), 0)
+        nc.vector.memset(mix_scale[:].bitcast(I32), 0)
+        for zeros in f1 + f2:
+            nc.vector.memset(zeros[:], 0.0)
+
+        def load_scale_rows(plane, rows):
+            for quad in range(4):
+                nc.sync.dma_start(
+                    plane[32 * quad : 32 * quad + 4, :].bitcast(I32), rows[4 * quad : 4 * quad + 4, :].bitcast(I32)
+                )
+
+        query_rows = query.rearrange("(p j) q -> p j q", j=PACK)
+        nc.sync.dma_start(raw[0][:], query_rows[:, :, 0 : Q // 2])
+        load_scale_rows(key_scale, keys_scales[0])
+        nc.sync.dma_start(raw[1][:], query_rows[:, :, Q // 2 : Q])
+        nc.sync.dma_start(key_words[:].bitcast(I32), keys_words[0].bitcast(I32))
+        for tile, src in zip(lists, (offs, offs2, offs3, offs4, offs5, offs6)):
+            nc.sync.dma_start(tile[:], src)
+        nc.sync.dma_start(row_factor[:], rowf.rearrange("(p r) one -> p (r one)", r=PACK))
+        nc.sync.dma_start(mix_codes[:].bitcast(I32), mix_words[0].rearrange("p n t -> p (n t)").bitcast(I32))
+        load_scale_rows(mix_scale, mix_scales[0])
+        idx, idx2, idx3, idx4, idx5, idx6 = lists
+
+        dealt = keep.tile([P, PACK * Q], BF16, align_bytes=64)
+        dealt_v = dealt[:].rearrange("p (r m j) -> p m j r", r=PACK, j=PACK)
+        half_m = P // 2
+
+        def deal(copy, c, r0, r1):
+            copy(
+                dealt_v[:, c * half_m : (c + 1) * half_m, :, r0:r1],
+                raw[c][:].rearrange("p j (m r) -> p m j r", r=PACK)[:, :, :, r0:r1],
+            )
+
+        q_codes = {}
+        q_scale = {}
+
+        def quantize_queries(r0, r1):
+            width = (r1 - r0) * P
+            codes = keep.tile([P, width], U32, align_bytes=64, name="q_codes%d" % r0)
+            scale = keep.tile([P, width], U8, align_bytes=64, name="q_scale%d" % r0)
+            nc.vector.quantize_mx(out=codes[:].bitcast(FP8X4), scales=scale[:], in_=dealt[:, r0 * Q : r1 * Q])
+            for r in range(r0, r1):
+                q_codes[r] = codes[:, (r - r0) * P : (r - r0 + 1) * P]
+                q_scale[r] = scale[:, (r - r0) * P : (r - r0 + 1) * P]
+
+        deal(nc.vector.tensor_copy, 0, 0, 2)
+        deal(nc.scalar.copy, 0, 2, 4)
+        deal(nc.vector.tensor_copy, 1, 0, 1)
+        deal(nc.vector.tensor_copy, 1, 1, 2)
+        quantize_queries(0, 1)
+        deal(nc.vector.tensor_copy, 1, 2, 4)
+        quantize_queries(1, 2)
+        quantize_queries(2, 4)
+
+        banks = [[psum.tile([P, BANK], F32, name="bank%d_%d" % (r, n)) for n in range(2)] for r in range(PACK)]
+        for r in range(PACK):
+            for n in range(2):
+                nc.tensor.matmul_mx(
+                    out=banks[r][n][:],
+                    lhsT=q_codes[r].bitcast(FP8X4),
+                    lhsT_scale=q_scale[r],
+                    rhs=key_words[:, 2 * n * BANK : 2 * (n + 1) * BANK].bitcast(FP4X4),
+                    rhs_scale=key_scale[:, n * BANK : (n + 1) * BANK],
+                    start=True,
+                    stop=True,
+                )
+
+        halves = [(slice(h * HALF, (h + 1) * HALF), slice(h * LIST_COLS // 2, (h + 1) * LIST_COLS // 2)) for h in range(2)]
+
+        c1 = []
+        for r in range(PACK):
+            if r == PACK - 1:
+                a = shared.tile([P, T], F32, name="a%d" % r, offset=0)
+            else:
+                a = keep.tile([P, T], F32, name="a%d" % r)
+            picked = keep.tile([P, I], F32, name="picked%d" % r)
+            placed = f1[r % 2]
+            nc.scalar.copy(a[:, 0:BANK], banks[r][0][:])
+            if r == 0:
+                nc.vector.tensor_copy(a[:, BANK:T], banks[r][1][:])
+                (slots_a, cols_a), (slots_b, cols_b) = halves
+                nc.vector.tensor_copy(picked[:, slots_a], a[:].indirect(idx[:, cols_a]))
+                nc.scalar.activation(picked[:, slots_b], a[:].indirect(idx[:, cols_b]), COPY)
+                for slots, cols in halves:
+                    nc.vector.tensor_copy(placed[:].indirect(idx2[:, cols]), picked[:, slots])
+            else:
+                nc.scalar.copy(a[:, BANK:T], banks[r][1][:])
+                nc.scalar.activation(picked[:], a[:].indirect(idx[:]), COPY)
+                nc.vector.tensor_copy(placed[:].indirect(idx2[:]), picked[:])
+            larger = keep.tile([P, T], F32, name="c1_%d" % r)
+            for n in range(2):
+                cols = slice(n * BANK, (n + 1) * BANK)
+                nc.vector.tensor_tensor(larger[:, cols], banks[r][n][:], placed[:, cols], ALU.max)
+            c1.append(larger)
+
+        w = []
+        for r in range(PACK):
+            at3 = shared.tile([P, I], F32, name="at3_%d" % r, offset=4 * I * (r % 2))
+            at4 = shared.tile([P, I], F32, name="at4_%d" % r, offset=4 * I * (2 + r % 2))
+            nc.scalar.activation(at3[:], c1[r][:].indirect(idx3[:]), COPY)
+            nc.scalar.activation(at4[:], c1[r][:].indirect(idx4[:]), COPY)
+            diff = keep.tile([P, I], F32, name="w%d" % r)
+            nc.gpsimd.tensor_tensor(diff[:], at3[:], at4[:], ALU.subtract)
+            w.append(diff)
+
+        gw = [keep.tile([P, HALF, PACK], BF16, align_bytes=64, name="gw%d" % h) for h in range(2)]
+        g = [keep.tile([P, I], F32, name="g%d" % r) for r in range(PACK)]
+
+        def scale_on_scalar(r, h):
+            nc.scalar.activation(gw[h][:, :, r], g[r][:, halves[h][0]], COPY, scale=row_factor[:, r : r + 1])
+
+        def scale_on_vector(r, h):
+            nc.vector.tensor_scalar(gw[h][:, :, r], g[r][:, halves[h][0]], row_factor[:, r : r + 1], None, ALU.mult)
+
+        last = PACK - 1
+        for r in range(PACK):
+            placed = f2[r % 2]
+            nc.vector.tensor_copy(placed[:].indirect(idx5[:]), w[r][:])
+            if r < 2:
+                c2 = shared.tile([P, T], F32, name="c2_%d" % r, offset=4 * T * r)
+            else:
+                c2 = keep.tile([P, T], F32, name="c2_%d" % r)
+            if r < last:
+                nc.gpsimd.tensor_tensor(c2[:], c1[r][:], placed[:], ALU.add)
+                nc.scalar.activation(g[r][:], c2[:].indirect(idx6[:]), COPY)
+                if r < 2:
+                    scale_on_scalar(r, 0)
+                scale_on_scalar(r, 1)
+            else:
+                nc.vector.tensor_tensor(c2[:], c1[r][:], placed[:], ALU.add)
+                scale_on_vector(r - 1, 0)
+                (slots_a, cols_a), (slots_b, cols_b) = halves
+                nc.vector.tensor_copy(g[r][:, slots_a], c2[:].indirect(idx6[:, cols_a]))
+                nc.scalar.activation(g[r][:, slots_b], c2[:].indirect(idx6[:, cols_b]), COPY)
+                scale_on_vector(r, 0)
+                scale_on_scalar(r, 1)
+
+        out_rows = out.rearrange("(e p) i -> p e i", p=P)
+        for h in range(2):
+            codes = keep.tile([P, HALF], U32, align_bytes=64, name="gw_codes%d" % h)
+            scale = keep.tile([P, HALF], U8, align_bytes=64, name="gw_scale%d" % h)
+            nc.vector.quantize_mx(
+                out=codes[:].bitcast(FP8X4), scales=scale[:], in_=gw[h][:].rearrange("p i r -> p (i r)")
+            )
+            staged = keep.tile([P, 2, HALF], F32, name="staged%d" % h)
+            for e in range(2):
+                bank = banks[h][e]
+                nc.tensor.matmul_mx(
+                    out=bank[:, 0:HALF],
+                    lhsT=mix_codes[:, e * P : (e + 1) * P].bitcast(FP8X4),
+                    lhsT_scale=mix_scale[:, e * P : (e + 1) * P],
+                    rhs=codes[:].bitcast(FP8X4),
+                    rhs_scale=scale[:],
+                    start=True,
+                    stop=True,
+                )
+                if e == 0:
+                    nc.scalar.copy(staged[:, e, :], bank[:, 0:HALF])
+                else:
+                    nc.vector.tensor_copy(staged[:, e, :], bank[:, 0:HALF])
+            nc.sync.dma_start(out_rows[:, :, halves[h][0]], staged[:])

@@ -21,6 +21,12 @@ PACK = 4
 BANK = 512
 HALF = I // 2
 LIST_COLS = I // 16
+KIB = 1024
+A_AT = (32, 0, 4, 14)
+C1_AT = (0, 4, 8, 36)
+PAIR_AT = (12, 16)
+C2_AT = (12, 16, 4, 44)
+F2_AT = (24, 28, 32)
 
 
 def tile_attend_hopmax_one_mixed_kernel(
@@ -39,12 +45,11 @@ def tile_attend_hopmax_one_mixed_kernel(
         mix_codes = keep.tile([P, E], U32, align_bytes=64)
         row_factor = keep.tile([P, PACK], F32)
         raw = [keep.tile([P, PACK, Q // 2], F32, name="raw%d" % c) for c in range(2)]
-        f1 = [keep.tile([P, T], F32, name="f1_%d" % b) for b in range(2)]
-        f2 = [keep.tile([P, T], F32, name="f2_%d" % b) for b in range(2)]
+        f1 = [keep.tile([P, T], F32, name="f1_%d" % b) for b in range(3)]
 
         nc.vector.memset(key_scale[:].bitcast(I32), 0)
         nc.vector.memset(mix_scale[:].bitcast(I32), 0)
-        for zeros in f1 + f2:
+        for zeros in f1:
             nc.vector.memset(zeros[:], 0.0)
 
         def load_scale_rows(plane, rows):
@@ -65,7 +70,7 @@ def tile_attend_hopmax_one_mixed_kernel(
         load_scale_rows(mix_scale, mix_scales[0])
         idx, idx2, idx3, idx4, idx5, idx6 = lists
 
-        dealt = keep.tile([P, PACK * Q], BF16, align_bytes=64)
+        dealt = shared.tile([P, PACK * Q], BF16, align_bytes=64, offset=26 * KIB)
         dealt_v = dealt[:].rearrange("p (r m j) -> p m j r", r=PACK, j=PACK)
         half_m = P // 2
 
@@ -111,44 +116,62 @@ def tile_attend_hopmax_one_mixed_kernel(
 
         halves = [(slice(h * HALF, (h + 1) * HALF), slice(h * LIST_COLS // 2, (h + 1) * LIST_COLS // 2)) for h in range(2)]
 
-        c1 = []
-        for r in range(PACK):
-            if r == PACK - 1:
-                a = shared.tile([P, T], F32, name="a%d" % r, offset=0)
-            else:
-                a = keep.tile([P, T], F32, name="a%d" % r)
+        (slots_a, cols_a), (slots_b, cols_b) = halves
+        last = PACK - 1
+        c1 = {}
+
+        def first_hop(r):
+            a = shared.tile([P, T], F32, name="a%d" % r, offset=A_AT[r] * KIB)
             picked = keep.tile([P, I], F32, name="picked%d" % r)
-            placed = f1[r % 2]
+            placed = f1[r % 3]
             nc.scalar.copy(a[:, 0:BANK], banks[r][0][:])
             if r == 0:
                 nc.vector.tensor_copy(a[:, BANK:T], banks[r][1][:])
-                (slots_a, cols_a), (slots_b, cols_b) = halves
                 nc.vector.tensor_copy(picked[:, slots_a], a[:].indirect(idx[:, cols_a]))
                 nc.scalar.activation(picked[:, slots_b], a[:].indirect(idx[:, cols_b]), COPY)
-                for slots, cols in halves:
+                for slots, cols in reversed(halves):
                     nc.vector.tensor_copy(placed[:].indirect(idx2[:, cols]), picked[:, slots])
             else:
                 nc.scalar.copy(a[:, BANK:T], banks[r][1][:])
                 nc.scalar.activation(picked[:], a[:].indirect(idx[:]), COPY)
                 nc.vector.tensor_copy(placed[:].indirect(idx2[:]), picked[:])
-            larger = keep.tile([P, T], F32, name="c1_%d" % r)
+
+        def take_larger(r):
+            c1[r] = shared.tile([P, T], F32, name="c1_%d" % r, offset=C1_AT[r] * KIB)
             for n in range(2):
                 cols = slice(n * BANK, (n + 1) * BANK)
-                nc.vector.tensor_tensor(larger[:, cols], banks[r][n][:], placed[:, cols], ALU.max)
-            c1.append(larger)
+                nc.vector.tensor_tensor(c1[r][:, cols], banks[r][n][:], f1[r % 3][:, cols], ALU.max)
 
-        w = []
-        for r in range(PACK):
-            at3 = shared.tile([P, I], F32, name="at3_%d" % r, offset=4 * I * (r % 2))
-            at4 = shared.tile([P, I], F32, name="at4_%d" % r, offset=4 * I * (2 + r % 2))
-            nc.scalar.activation(at3[:], c1[r][:].indirect(idx3[:]), COPY)
-            nc.scalar.activation(at4[:], c1[r][:].indirect(idx4[:]), COPY)
-            diff = keep.tile([P, I], F32, name="w%d" % r)
-            nc.gpsimd.tensor_tensor(diff[:], at3[:], at4[:], ALU.subtract)
-            w.append(diff)
+        first_hop(0)
+        first_hop(1)
+        take_larger(0)
+        first_hop(2)
+        take_larger(1)
+        take_larger(2)
+        first_hop(3)
+        take_larger(3)
 
+        f2 = [shared.tile([P, T], F32, name="f2_%d" % b, offset=F2_AT[b] * KIB) for b in range(3)]
+        for zeros in f2:
+            nc.gpsimd.memset(zeros[:], 0.0)
+
+        w = {}
+        c2 = {}
         gw = [keep.tile([P, HALF, PACK], BF16, align_bytes=64, name="gw%d" % h) for h in range(2)]
-        g = [keep.tile([P, I], F32, name="g%d" % r) for r in range(PACK)]
+        g = [keep.tile([P, I], F32, name="g%d" % r) for r in range(last)]
+
+        def difference(r):
+            pair = shared.tile([P, 2 * I], F32, name="pair%d" % r, offset=PAIR_AT[r % 2] * KIB)
+            nc.scalar.activation(pair[:, 0:I], c1[r][:].indirect(idx3[:]), COPY)
+            nc.scalar.activation(pair[:, I : 2 * I], c1[r][:].indirect(idx4[:]), COPY)
+            w[r] = keep.tile([P, I], F32, name="w%d" % r)
+            nc.gpsimd.tensor_tensor(w[r][:], pair[:, 0:I], pair[:, I : 2 * I], ALU.subtract)
+
+        def add_placed(r, add):
+            placed = f2[r % 3]
+            nc.vector.tensor_copy(placed[:].indirect(idx5[:]), w[r][:])
+            c2[r] = shared.tile([P, T], F32, name="c2_%d" % r, offset=C2_AT[r] * KIB)
+            add(c2[r][:], c1[r][:], placed[:], ALU.add)
 
         def scale_on_scalar(r, h):
             nc.scalar.activation(gw[h][:, :, r], g[r][:, halves[h][0]], COPY, scale=row_factor[:, r : r + 1])
@@ -156,38 +179,33 @@ def tile_attend_hopmax_one_mixed_kernel(
         def scale_on_vector(r, h):
             nc.vector.tensor_scalar(gw[h][:, :, r], g[r][:, halves[h][0]], row_factor[:, r : r + 1], None, ALU.mult)
 
-        last = PACK - 1
-        for r in range(PACK):
-            placed = f2[r % 2]
-            nc.vector.tensor_copy(placed[:].indirect(idx5[:]), w[r][:])
+        for r in range(last):
+            difference(r)
+        add_placed(0, nc.gpsimd.tensor_tensor)
+        difference(last)
+        for r in range(last):
+            if r > 0:
+                add_placed(r, nc.gpsimd.tensor_tensor)
+            nc.scalar.activation(g[r][:], c2[r][:].indirect(idx6[:]), COPY)
             if r < 2:
-                c2 = shared.tile([P, T], F32, name="c2_%d" % r, offset=4 * T * r)
-            else:
-                c2 = keep.tile([P, T], F32, name="c2_%d" % r)
-            if r < last:
-                nc.gpsimd.tensor_tensor(c2[:], c1[r][:], placed[:], ALU.add)
-                nc.scalar.activation(g[r][:], c2[:].indirect(idx6[:]), COPY)
-                if r < 2:
-                    scale_on_scalar(r, 0)
-                scale_on_scalar(r, 1)
-            else:
-                nc.vector.tensor_tensor(c2[:], c1[r][:], placed[:], ALU.add)
-                scale_on_vector(r - 1, 0)
-                (slots_a, cols_a), (slots_b, cols_b) = halves
-                nc.vector.tensor_copy(g[r][:, slots_a], c2[:].indirect(idx6[:, cols_a]))
-                nc.scalar.activation(g[r][:, slots_b], c2[:].indirect(idx6[:, cols_b]), COPY)
-                scale_on_vector(r, 0)
-                scale_on_scalar(r, 1)
+                scale_on_scalar(r, 0)
+            scale_on_scalar(r, 1)
+        add_placed(last, nc.vector.tensor_tensor)
+        scale_on_vector(last - 1, 0)
+        g.append(shared.tile([P, I], F32, name="g%d" % last, offset=C2_AT[last - 1] * KIB))
+        nc.scalar.activation(g[last][:, slots_a], c2[last][:].indirect(idx6[:, cols_a]), COPY)
+        nc.vector.tensor_copy(g[last][:, slots_b], c2[last][:].indirect(idx6[:, cols_b]))
+        scale_on_vector(last, 0)
+        scale_on_scalar(last, 1)
 
-        out_rows = out.rearrange("(e p) i -> p e i", p=P)
         for h in range(2):
             codes = keep.tile([P, HALF], U32, align_bytes=64, name="gw_codes%d" % h)
             scale = keep.tile([P, HALF], U8, align_bytes=64, name="gw_scale%d" % h)
             nc.vector.quantize_mx(
                 out=codes[:].bitcast(FP8X4), scales=scale[:], in_=gw[h][:].rearrange("p i r -> p (i r)")
             )
-            staged = keep.tile([P, 2, HALF], F32, name="staged%d" % h)
             for e in range(2):
+                staged = keep.tile([P, HALF], F32, name="staged%d_%d" % (h, e))
                 bank = banks[h][e]
                 nc.tensor.matmul_mx(
                     out=bank[:, 0:HALF],
@@ -199,7 +217,7 @@ def tile_attend_hopmax_one_mixed_kernel(
                     stop=True,
                 )
                 if e == 0:
-                    nc.scalar.copy(staged[:, e, :], bank[:, 0:HALF])
+                    nc.scalar.copy(staged[:], bank[:, 0:HALF])
                 else:
-                    nc.vector.tensor_copy(staged[:, e, :], bank[:, 0:HALF])
-            nc.sync.dma_start(out_rows[:, :, halves[h][0]], staged[:])
+                    nc.vector.tensor_copy(staged[:], bank[:, 0:HALF])
+                nc.sync.dma_start(out[e * P : (e + 1) * P, halves[h][0]], staged[:])

@@ -60,8 +60,8 @@ def tile_attend_hopmax_one_mixed_kernel(
 
         query_rows = query.rearrange("(p j) q -> p j q", j=PACK)
         nc.sync.dma_start(raw[0][:], query_rows[:, :, 0 : Q // 2])
-        load_scale_rows(key_scale, keys_scales[0])
         nc.sync.dma_start(raw[1][:], query_rows[:, :, Q // 2 : Q])
+        load_scale_rows(key_scale, keys_scales[0])
         nc.sync.dma_start(key_words[:].bitcast(I32), keys_words[0].bitcast(I32))
         for tile, src in zip(lists, (offs, offs2, offs3, offs4, offs5, offs6)):
             nc.sync.dma_start(tile[:], src)
@@ -74,10 +74,10 @@ def tile_attend_hopmax_one_mixed_kernel(
         dealt_v = dealt[:].rearrange("p (r m j) -> p m j r", r=PACK, j=PACK)
         half_m = P // 2
 
-        def deal(copy, c, r0, r1):
+        def deal(copy, c, r0, r1, m0=0, m1=half_m):
             copy(
-                dealt_v[:, c * half_m : (c + 1) * half_m, :, r0:r1],
-                raw[c][:].rearrange("p j (m r) -> p m j r", r=PACK)[:, :, :, r0:r1],
+                dealt_v[:, c * half_m + m0 : c * half_m + m1, :, r0:r1],
+                raw[c][:].rearrange("p j (m r) -> p m j r", r=PACK)[:, m0:m1, :, r0:r1],
             )
 
         q_codes = {}
@@ -95,9 +95,8 @@ def tile_attend_hopmax_one_mixed_kernel(
         deal(nc.vector.tensor_copy, 0, 0, 2)
         deal(nc.scalar.copy, 0, 2, 4)
         deal(nc.vector.tensor_copy, 1, 0, 1)
-        deal(nc.vector.tensor_copy, 1, 1, 2)
+        deal(nc.scalar.copy, 1, 1, 4)
         quantize_queries(0, 1)
-        deal(nc.vector.tensor_copy, 1, 2, 4)
         quantize_queries(1, 2)
         quantize_queries(2, 4)
 
@@ -189,12 +188,13 @@ def tile_attend_hopmax_one_mixed_kernel(
             nc.scalar.activation(g[r][:], c2[r][:].indirect(idx6[:]), COPY)
             if r < 2:
                 scale_on_scalar(r, 0)
-            scale_on_scalar(r, 1)
+                scale_on_scalar(r, 1)
         add_placed(last, nc.vector.tensor_tensor)
         scale_on_vector(last - 1, 0)
         g.append(shared.tile([P, I], F32, name="g%d" % last, offset=C2_AT[last - 1] * KIB))
         nc.scalar.activation(g[last][:, slots_a], c2[last][:].indirect(idx6[:, cols_a]), COPY)
         nc.vector.tensor_copy(g[last][:, slots_b], c2[last][:].indirect(idx6[:, cols_b]))
+        scale_on_scalar(last - 1, 1)
         scale_on_vector(last, 0)
         scale_on_scalar(last, 1)
 

@@ -53,10 +53,8 @@ def tile_attend_hopmax_one_mixed_kernel(
             nc.vector.memset(zeros[:], 0.0)
 
         def load_scale_rows(plane, rows):
-            for quad in range(4):
-                nc.sync.dma_start(
-                    plane[32 * quad : 32 * quad + 4, :].bitcast(I32), rows[4 * quad : 4 * quad + 4, :].bitcast(I32)
-                )
+            for f in range(4):
+                nc.sync.dma_start(plane[f:P:32, :].bitcast(I32), rows[f:16:4, :].bitcast(I32))
 
         query_rows = query.rearrange("(p j) q -> p j q", j=PACK)
         nc.sync.dma_start(raw[0][:], query_rows[:, :, 0 : Q // 2])
@@ -71,13 +69,13 @@ def tile_attend_hopmax_one_mixed_kernel(
         idx, idx2, idx3, idx4, idx5, idx6 = lists
 
         dealt = shared.tile([P, PACK * Q], BF16, align_bytes=64, offset=26 * KIB)
-        dealt_v = dealt[:].rearrange("p (r m j) -> p m j r", r=PACK, j=PACK)
+        dealt_v = dealt[:].rearrange("p (r m j) -> p r m j", r=PACK, j=PACK)
         half_m = P // 2
 
-        def deal(copy, c, r0, r1, m0=0, m1=half_m):
+        def deal(copy, c, r0, r1):
             copy(
-                dealt_v[:, c * half_m + m0 : c * half_m + m1, :, r0:r1],
-                raw[c][:].rearrange("p j (m r) -> p m j r", r=PACK)[:, m0:m1, :, r0:r1],
+                dealt_v[:, r0:r1, c * half_m : (c + 1) * half_m, :],
+                raw[c][:].rearrange("p j (m r) -> p r m j", r=PACK)[:, r0:r1, :, :],
             )
 
         q_codes = {}
@@ -95,8 +93,10 @@ def tile_attend_hopmax_one_mixed_kernel(
         deal(nc.vector.tensor_copy, 0, 0, 2)
         deal(nc.scalar.copy, 0, 2, 4)
         deal(nc.vector.tensor_copy, 1, 0, 1)
-        deal(nc.scalar.copy, 1, 1, 4)
+        deal(nc.vector.tensor_copy, 1, 1, 2)
+        deal(nc.scalar.copy, 1, 3, 4)
         quantize_queries(0, 1)
+        deal(nc.vector.tensor_copy, 1, 2, 3)
         quantize_queries(1, 2)
         quantize_queries(2, 4)
 

@@ -44,7 +44,7 @@ def tile_attend_hopmax_one_mixed_kernel(
         mix_scale = keep.tile([P, E], U8, align_bytes=64)
         mix_codes = keep.tile([P, E], U32, align_bytes=64)
         row_factor = keep.tile([P, PACK], F32)
-        raw = [keep.tile([P, PACK, Q // 2], F32, name="raw%d" % c) for c in range(2)]
+        raw = [keep.tile([P, 2, Q], F32, name="raw%d" % c) for c in range(2)]
         f1 = [keep.tile([P, T], F32, name="f1_%d" % b) for b in range(3)]
 
         nc.vector.memset(key_scale[:].bitcast(I32), 0)
@@ -57,10 +57,10 @@ def tile_attend_hopmax_one_mixed_kernel(
                 nc.sync.dma_start(plane[f:P:32, :].bitcast(I32), rows[f:16:4, :].bitcast(I32))
 
         query_rows = query.rearrange("(p j) q -> p j q", j=PACK)
-        nc.sync.dma_start(raw[0][:], query_rows[:, :, 0 : Q // 2])
-        nc.sync.dma_start(raw[1][:], query_rows[:, :, Q // 2 : Q])
-        load_scale_rows(key_scale, keys_scales[0])
+        nc.sync.dma_start(raw[0][:], query_rows[:, 0:2, :])
+        nc.sync.dma_start(raw[1][:], query_rows[:, 2:4, :])
         nc.sync.dma_start(key_words[:].bitcast(I32), keys_words[0].bitcast(I32))
+        load_scale_rows(key_scale, keys_scales[0])
         for tile, src in zip(lists, (offs, offs2, offs3, offs4, offs5, offs6)):
             nc.sync.dma_start(tile[:], src)
         nc.sync.dma_start(row_factor[:], rowf.rearrange("(p r) one -> p (r one)", r=PACK))
@@ -70,11 +70,10 @@ def tile_attend_hopmax_one_mixed_kernel(
 
         dealt = shared.tile([P, PACK * Q], BF16, align_bytes=64, offset=26 * KIB)
         dealt_v = dealt[:].rearrange("p (r m j) -> p r m j", r=PACK, j=PACK)
-        half_m = P // 2
 
         def deal(copy, c, r0, r1):
             copy(
-                dealt_v[:, r0:r1, c * half_m : (c + 1) * half_m, :],
+                dealt_v[:, r0:r1, :, 2 * c : 2 * c + 2],
                 raw[c][:].rearrange("p j (m r) -> p r m j", r=PACK)[:, r0:r1, :, :],
             )
 
@@ -94,21 +93,27 @@ def tile_attend_hopmax_one_mixed_kernel(
         deal(nc.scalar.copy, 0, 2, 4)
         deal(nc.vector.tensor_copy, 1, 0, 1)
         deal(nc.vector.tensor_copy, 1, 1, 2)
-        deal(nc.scalar.copy, 1, 3, 4)
+        deal(nc.scalar.copy, 1, 2, 4)
         quantize_queries(0, 1)
-        deal(nc.vector.tensor_copy, 1, 2, 3)
         quantize_queries(1, 2)
         quantize_queries(2, 4)
 
-        banks = [[psum.tile([P, BANK], F32, name="bank%d_%d" % (r, n)) for n in range(2)] for r in range(PACK)]
-        for r in range(PACK):
-            for n in range(2):
+        banks = [psum.tile([P, BANK], F32, name="bank%d" % n) for n in range(8)]
+        pieces = {
+            0: [(0, 0, 512), (1, 512, 768), (2, 768, 1024)],
+            1: [(3, 0, 512), (4, 512, 1024)],
+            2: [(5, 0, 512), (6, 512, 1024)],
+            3: [(7, 0, 512), (0, 512, 1024)],
+        }
+
+        def score(r):
+            for n, t0, t1 in pieces[r]:
                 nc.tensor.matmul_mx(
-                    out=banks[r][n][:],
+                    out=banks[n][:, 0 : t1 - t0],
                     lhsT=q_codes[r].bitcast(FP8X4),
                     lhsT_scale=q_scale[r],
-                    rhs=key_words[:, 2 * n * BANK : 2 * (n + 1) * BANK].bitcast(FP4X4),
-                    rhs_scale=key_scale[:, n * BANK : (n + 1) * BANK],
+                    rhs=key_words[:, 2 * t0 : 2 * t1].bitcast(FP4X4),
+                    rhs_scale=key_scale[:, t0:t1],
                     start=True,
                     stop=True,
                 )
@@ -118,28 +123,33 @@ def tile_attend_hopmax_one_mixed_kernel(
         (slots_a, cols_a), (slots_b, cols_b) = halves
         last = PACK - 1
         c1 = {}
+        scores = {}
 
         def first_hop(r):
             a = shared.tile([P, T], F32, name="a%d" % r, offset=A_AT[r] * KIB)
             picked = keep.tile([P, I], F32, name="picked%d" % r)
             placed = f1[r % 3]
-            nc.scalar.copy(a[:, 0:BANK], banks[r][0][:])
+            scores[r] = a
+            score(r)
+            for n, t0, t1 in pieces[r]:
+                copy = nc.vector.tensor_copy if (r == 0 and t1 == T) else nc.scalar.copy
+                copy(a[:, t0:t1], banks[n][:, 0 : t1 - t0])
             if r == 0:
-                nc.vector.tensor_copy(a[:, BANK:T], banks[r][1][:])
                 nc.vector.tensor_copy(picked[:, slots_a], a[:].indirect(idx[:, cols_a]))
                 nc.scalar.activation(picked[:, slots_b], a[:].indirect(idx[:, cols_b]), COPY)
                 for slots, cols in reversed(halves):
                     nc.vector.tensor_copy(placed[:].indirect(idx2[:, cols]), picked[:, slots])
             else:
-                nc.scalar.copy(a[:, BANK:T], banks[r][1][:])
                 nc.scalar.activation(picked[:], a[:].indirect(idx[:]), COPY)
                 nc.vector.tensor_copy(placed[:].indirect(idx2[:]), picked[:])
 
         def take_larger(r):
             c1[r] = shared.tile([P, T], F32, name="c1_%d" % r, offset=C1_AT[r] * KIB)
-            for n in range(2):
-                cols = slice(n * BANK, (n + 1) * BANK)
-                nc.vector.tensor_tensor(c1[r][:, cols], banks[r][n][:], f1[r % 3][:, cols], ALU.max)
+            if r == 0:
+                nc.vector.tensor_tensor(c1[r][:], scores[r][:], f1[r % 3][:], ALU.max)
+            else:
+                for n, t0, t1 in pieces[r]:
+                    nc.vector.tensor_tensor(c1[r][:, t0:t1], banks[n][:], f1[r % 3][:, t0:t1], ALU.max)
 
         first_hop(0)
         first_hop(1)
@@ -206,7 +216,7 @@ def tile_attend_hopmax_one_mixed_kernel(
             )
             for e in range(2):
                 staged = keep.tile([P, HALF], F32, name="staged%d_%d" % (h, e))
-                bank = banks[h][e]
+                bank = banks[1 + 2 * h + e]
                 nc.tensor.matmul_mx(
                     out=bank[:, 0:HALF],
                     lhsT=mix_codes[:, e * P : (e + 1) * P].bitcast(FP8X4),

from contextlib import ExitStack

import concourse.mybir as mybir

D, T, I, Q, E = 512, 1024, 512, 512, 256
FLOPS = 2 * D * Q * T + 2 * Q * E * I

F32 = mybir.dt.float32
BF16 = mybir.dt.bfloat16
I32 = mybir.dt.int32
U32 = mybir.dt.uint32
U16 = mybir.dt.uint16
U8 = mybir.dt.uint8
FP8X4 = mybir.dt.float8_e4m3fn_x4
FP4X4 = mybir.dt.float4_e2m1fn_x4
ALU = mybir.AluOpType
COPY = mybir.ActivationFunctionType.Copy

P = 128
PACK = 4
BANK = 512
HALF = I // 2
LIST_COLS = I // 16
KIB = 1024
A_AT = (32, 0, 4, 14)
C1_AT = (0, 4, 8, 36)
PAIR_AT = (12, 16)
C2_AT = (12, 16, 4, 44)
F2_AT = (24, 28, 32)


def tile_attend_hopmax_one_mixed_kernel(
    tc, query, keys_words, keys_scales, rowf, mix_words, mix_scales, offs, offs2, offs3, offs4, offs5, offs6, out
):
    nc = tc.nc
    with ExitStack() as ctx:
        keep = ctx.enter_context(tc.tile_pool(name="keep", bufs=1))
        shared = ctx.enter_context(tc.tile_pool(name="shared", bufs=1))
        psum = ctx.enter_context(tc.psum_pool(name="psum", bufs=1))

        lists = [keep.tile([P, LIST_COLS], U16, name="list%d" % n) for n in range(6)]
        key_scale = keep.tile([P, T], U8, align_bytes=64)
        key_words = keep.tile([P, 2 * T], U8, align_bytes=64)
        mix_scale = keep.tile([P, E], U8, align_bytes=64)
        mix_codes = keep.tile([P, E], U32, align_bytes=64)
        row_factor = keep.tile([P, PACK], F32)
        raw = [keep.tile([P, 2, Q], F32, name="raw%d" % c) for c in range(2)]
        f1 = [keep.tile([P, T], F32, name="f1_%d" % b) for b in range(3)]

        nc.vector.memset(key_scale[:].bitcast(I32), 0)
        nc.vector.memset(mix_scale[:].bitcast(I32), 0)
        for zeros in f1:
            nc.vector.memset(zeros[:], 0.0)

        def load_scale_rows(plane, rows):
            for f in range(4):
                nc.sync.dma_start(plane[f:P:32, :].bitcast(I32), rows[f:16:4, :].bitcast(I32))

        query_rows = query.rearrange("(p j) q -> p j q", j=PACK)
        nc.sync.dma_start(raw[0][:], query_rows[:, 0:2, :])
        nc.sync.dma_start(raw[1][:], query_rows[:, 2:4, :])
        nc.sync.dma_start(key_words[:].bitcast(I32), keys_words[0].bitcast(I32))
        load_scale_rows(key_scale, keys_scales[0])
        for tile, src in zip(lists, (offs, offs2, offs3, offs4, offs5, offs6)):
            nc.sync.dma_start(tile[:], src)
        nc.sync.dma_start(row_factor[:], rowf.rearrange("(p r) one -> p (r one)", r=PACK))
        nc.sync.dma_start(mix_codes[:].bitcast(I32), mix_words[0].rearrange("p n t -> p (n t)").bitcast(I32))
        load_scale_rows(mix_scale, mix_scales[0])
        idx, idx2, idx3, idx4, idx5, idx6 = lists

        dealt = shared.tile([P, PACK * Q], BF16, align_bytes=64, offset=26 * KIB)
        dealt_v = dealt[:].rearrange("p (r m j) -> p r m j", r=PACK, j=PACK)

        def deal(copy, c, r0, r1):
            copy(
                dealt_v[:, r0:r1, :, 2 * c : 2 * c + 2],
                raw[c][:].rearrange("p j (m r) -> p r m j", r=PACK)[:, r0:r1, :, :],
            )

        q_codes = {}
        q_scale = {}

        def quantize_queries(r0, r1):
            width = (r1 - r0) * P
            codes = keep.tile([P, width], U32, align_bytes=64, name="q_codes%d" % r0)
            scale = keep.tile([P, width], U8, align_bytes=64, name="q_scale%d" % r0)
            nc.vector.quantize_mx(out=codes[:].bitcast(FP8X4), scales=scale[:], in_=dealt[:, r0 * Q : r1 * Q])
            for r in range(r0, r1):
                q_codes[r] = codes[:, (r - r0) * P : (r - r0 + 1) * P]
                q_scale[r] = scale[:, (r - r0) * P : (r - r0 + 1) * P]

        deal(nc.vector.tensor_copy, 0, 0, 2)
        deal(nc.scalar.copy, 0, 2, 4)
        deal(nc.vector.tensor_copy, 1, 0, 1)
        deal(nc.vector.tensor_copy, 1, 1, 2)
        deal(nc.scalar.copy, 1, 2, 4)
        quantize_queries(0, 1)
        quantize_queries(1, 2)
        quantize_queries(2, 4)

        banks = [psum.tile([P, BANK], F32, name="bank%d" % n) for n in range(8)]
        pieces = {
            0: [(0, 0, 512), (1, 512, 768), (2, 768, 1024)],
            1: [(3, 0, 512), (4, 512, 1024)],
            2: [(5, 0, 512), (6, 512, 1024)],
            3: [(7, 0, 512), (0, 512, 1024)],
        }

        def score(r):
            for n, t0, t1 in pieces[r]:
                nc.tensor.matmul_mx(
                    out=banks[n][:, 0 : t1 - t0],
                    lhsT=q_codes[r].bitcast(FP8X4),
                    lhsT_scale=q_scale[r],
                    rhs=key_words[:, 2 * t0 : 2 * t1].bitcast(FP4X4),
                    rhs_scale=key_scale[:, t0:t1],
                    start=True,
                    stop=True,
                )

        halves = [(slice(h * HALF, (h + 1) * HALF), slice(h * LIST_COLS // 2, (h + 1) * LIST_COLS // 2)) for h in range(2)]

        (slots_a, cols_a), (slots_b, cols_b) = halves
        last = PACK - 1
        c1 = {}
        scores = {}

        def first_hop(r):
            a = shared.tile([P, T], F32, name="a%d" % r, offset=A_AT[r] * KIB)
            picked = keep.tile([P, I], F32, name="picked%d" % r)
            placed = f1[r % 3]
            scores[r] = a
            score(r)
            for n, t0, t1 in pieces[r]:
                copy = nc.vector.tensor_copy if (r == 0 and t1 == T) else nc.scalar.copy
                copy(a[:, t0:t1], banks[n][:, 0 : t1 - t0])
            if r == 0:
                nc.vector.tensor_copy(picked[:, slots_a], a[:].indirect(idx[:, cols_a]))
                nc.scalar.activation(picked[:, slots_b], a[:].indirect(idx[:, cols_b]), COPY)
                for slots, cols in reversed(halves):
                    nc.vector.tensor_copy(placed[:].indirect(idx2[:, cols]), picked[:, slots])
            else:
                nc.scalar.activation(picked[:], a[:].indirect(idx[:]), COPY)
                nc.vector.tensor_copy(placed[:].indirect(idx2[:]), picked[:])

        def take_larger(r):
            c1[r] = shared.tile([P, T], F32, name="c1_%d" % r, offset=C1_AT[r] * KIB)
            if r == 0:
                nc.vector.tensor_tensor(c1[r][:], scores[r][:], f1[r % 3][:], ALU.max)
            else:
                for n, t0, t1 in pieces[r]:
                    nc.vector.tensor_tensor(c1[r][:, t0:t1], banks[n][:], f1[r % 3][:, t0:t1], ALU.max)

        first_hop(0)
        first_hop(1)
        take_larger(0)
        first_hop(2)
        take_larger(1)
        take_larger(2)
        first_hop(3)
        take_larger(3)

        f2 = [shared.tile([P, T], F32, name="f2_%d" % b, offset=F2_AT[b] * KIB) for b in range(3)]
        for zeros in f2:
            nc.gpsimd.memset(zeros[:], 0.0)

        w = {}
        c2 = {}
        gw = [keep.tile([P, HALF, PACK], BF16, align_bytes=64, name="gw%d" % h) for h in range(2)]
        g = [keep.tile([P, I], F32, name="g%d" % r) for r in range(last)]

        def difference(r):
            pair = shared.tile([P, 2 * I], F32, name="pair%d" % r, offset=PAIR_AT[r % 2] * KIB)
            nc.scalar.activation(pair[:, 0:I], c1[r][:].indirect(idx3[:]), COPY)
            nc.scalar.activation(pair[:, I : 2 * I], c1[r][:].indirect(idx4[:]), COPY)
            w[r] = keep.tile([P, I], F32, name="w%d" % r)
            nc.gpsimd.tensor_tensor(w[r][:], pair[:, 0:I], pair[:, I : 2 * I], ALU.subtract)

        def add_placed(r, add):
            placed = f2[r % 3]
            nc.vector.tensor_copy(placed[:].indirect(idx5[:]), w[r][:])
            c2[r] = shared.tile([P, T], F32, name="c2_%d" % r, offset=C2_AT[r] * KIB)
            add(c2[r][:], c1[r][:], placed[:], ALU.add)

        def scale_on_scalar(r, h):
            nc.scalar.activation(gw[h][:, :, r], g[r][:, halves[h][0]], COPY, scale=row_factor[:, r : r + 1])

        def scale_on_vector(r, h):
            nc.vector.tensor_scalar(gw[h][:, :, r], g[r][:, halves[h][0]], row_factor[:, r : r + 1], None, ALU.mult)

        for r in range(last):
            difference(r)
        add_placed(0, nc.gpsimd.tensor_tensor)
        difference(last)
        for r in range(last):
            if r > 0:
                add_placed(r, nc.gpsimd.tensor_tensor)
            nc.scalar.activation(g[r][:], c2[r][:].indirect(idx6[:]), COPY)
            if r < 2:
                scale_on_scalar(r, 0)
                scale_on_scalar(r, 1)
        add_placed(last, nc.vector.tensor_tensor)
        scale_on_vector(last - 1, 0)
        g.append(shared.tile([P, I], F32, name="g%d" % last, offset=C2_AT[last - 1] * KIB))
        nc.scalar.activation(g[last][:, slots_a], c2[last][:].indirect(idx6[:, cols_a]), COPY)
        nc.vector.tensor_copy(g[last][:, slots_b], c2[last][:].indirect(idx6[:, cols_b]))
        scale_on_scalar(last - 1, 1)
        scale_on_vector(last, 0)
        scale_on_scalar(last, 1)

        for h in range(2):
            codes = keep.tile([P, HALF], U32, align_bytes=64, name="gw_codes%d" % h)
            scale = keep.tile([P, HALF], U8, align_bytes=64, name="gw_scale%d" % h)
            nc.vector.quantize_mx(
                out=codes[:].bitcast(FP8X4), scales=scale[:], in_=gw[h][:].rearrange("p i r -> p (i r)")
            )
            for e in range(2):
                staged = keep.tile([P, HALF], F32, name="staged%d_%d" % (h, e))
                bank = banks[1 + 2 * h + e]
                nc.tensor.matmul_mx(
                    out=bank[:, 0:HALF],
                    lhsT=mix_codes[:, e * P : (e + 1) * P].bitcast(FP8X4),
                    lhsT_scale=mix_scale[:, e * P : (e + 1) * P],
                    rhs=codes[:].bitcast(FP8X4),
                    rhs_scale=scale[:],
                    start=True,
                    stop=True,
                )
                if e == 0:
                    nc.scalar.copy(staged[:], bank[:, 0:HALF])
                else:
                    nc.vector.tensor_copy(staged[:], bank[:, 0:HALF])
                nc.sync.dma_start(out[e * P : (e + 1) * P, halves[h][0]], staged[:])
